import numpy as np, ml_dtypes
CORES = [26,28,98,100,106,108,122,124]
N = 8
TK, LAY = 256, 3
def setup_inputs(rng):
    return {"x": rng.standard_normal((N, 128, TK), dtype=np.float32).astype(ml_dtypes.bfloat16), "wu": (rng.standard_normal((N, 128, LAY * 256), dtype=np.float32) / 16).astype(ml_dtypes.bfloat16), "wd": (rng.standard_normal((N, 128, 256), dtype=np.float32) / 16).astype(ml_dtypes.bfloat16)}
def setup_inputs_big(rng):
    d = setup_inputs(rng)
    for k in ("x",): d[k] = (d[k].astype(np.float32) * 1048576.0).astype(d[k].dtype)
    return d
def setup_inputs_small(rng):
    d = setup_inputs(rng)
    for k in ("x",): d[k] = (d[k].astype(np.float32) * (1 / 1048576.0)).astype(d[k].dtype)
    return d
def setup_inputs_apart(rng):
    d = setup_inputs(rng)
    f = (10.0 ** rng.permutation(np.linspace(-1.5, 1.5, N))).astype(np.float32).reshape(N, 1, 1)
    for k in ("x",): d[k] = (d[k].astype(np.float32) * f).astype(d[k].dtype)
    return d
def reference(x, wu, wd):
    X, WU, WD = x.astype(np.float64), wu.astype(np.float64), wd.astype(np.float64)
    s = list(X)
    for l in range(LAY):
        for q in range(0, N, 2 << l):
            p = q + (1 << l)
            s[q] = np.maximum(WU[q][:, 256 * l:256 * l + 128].T @ s[q] + WU[q][:, 256 * l + 128:256 * l + 256].T @ s[p], 0.0)
    for l in range(LAY - 1, -1, -1):
        for q in range(0, N, 2 << l):
            p = q + (1 << l)
            s[p] = np.maximum(WD[p][:, 0:128].T @ s[p] + WD[p][:, 128:256].T @ s[q], 0.0)
    return {"y": np.stack(s).astype(ml_dtypes.bfloat16)}

from concourse.bass import DstId, RemoteDMATransfer
from concourse.mybir import AluOpType

N = 8
TK = 256
HF = 128


def _sb(cols, dtype="bfloat16"):
    return ("sbuf", [128, cols], dtype)


SCRATCH = {
    "xs": _sb(TK),
    "xp": _sb(TK),
    "wus": _sb(3 * TK),
    "wds": _sb(TK),
    "w12": _sb(2 * TK),
    "wd4": _sb(TK),
    "wde": _sb(TK),
    "ao": _sb(TK),
    "ae": _sb(TK),
    "b0": _sb(TK),
    "b4": _sb(TK),
    "a": _sb(TK), "b": _sb(TK), "c": _sb(TK), "y4": _sb(TK), "ye": _sb(TK), "yo": _sb(TK),
    "zero": _sb(HF, "float32"),
}
for _i in range(8):
    SCRATCH["p%d" % _i] = ("psum", [128, 512], "float32")

_STEPS = ("a", "b", "c", "4", "e", "y")
SEMAPHORES = [
    "ld_x", "ld_w0", "ld_w2", "ld_wd",
    "r_x", "r_a", "r_ae", "r_w1", "r_w2", "r_wd4", "r_wde", "r_b0", "r_b4",
    "z", "sent", "st",
]
SEMAPHORES += ["m_%s%d" % (s, h) for s in _STEPS for h in (0, 1)]
SEMAPHORES += ["v_%s%d" % (s, h) for s in _STEPS for h in (0, 1)]


def _bits(m):
    return [i for i in range(m.bit_length()) if (m >> i) & 1]


def _engines(topo, cores, src, dst, kind):
    full = topo.mask(src, dst)
    if topo.chip(src) != topo.chip(dst) or kind == "all":
        return full
    if kind == "spread":
        return sum(1 << b for b in _bits(full)[::2])
    far = [c for c in cores if topo.chip(c) != topo.chip(src)][0]
    return full & ~topo.mask(src, far)


def _links(topo, a, b):
    ca, cb = topo.chip(a), topo.chip(b)
    if ca == cb:
        return 0
    return 1 if (topo.mates(ca, cb) or topo.same_plane(ca, cb)) else 2


def _plan(cores, topo):
    calls = [[] for _ in range(N)]
    va, vb = ["v_a0", "v_a1"], ["v_b0", "v_b1"]

    def add(r, waits, *trs):
        calls[r].append((waits, trs))

    def tile(src, dst, sem, ranks, kind):
        return (src, 0, dst, 0, TK, sem, ranks, kind)

    def serve(holders, chips):
        def cost(cs):
            return sum(_links(topo, cores[h], cores[c[0]]) for h, c in zip(holders, cs))
        return dict(zip(holders, chips if cost(chips) <= cost(chips[::-1]) else chips[::-1]))

    to = serve((0, 2), ((5, 4), (7, 6)))
    to.update(serve((4, 6), ((1, 0), (3, 2))))

    add(0, ["ld_w2"], ("wus", 2 * TK, "w12", TK, TK, "r_w2", [1], "near"))
    add(0, ["ld_w0"], ("wus", TK, "w12", 0, 2 * TK, "r_w1", [2], "far"))
    add(4, ["ld_wd"], tile("wds", "wd4", "r_wd4", [5], "near"))
    add(4, ["ld_w0"], ("wus", TK, "w12", 0, TK, "r_w1", [6], "far"))
    for q in (2, 6):
        add(q, ["ld_wd"], tile("wds", "wde", "r_wde", [q + 1], "all"))
    for p in (1, 3, 5, 7):
        add(p, ["ld_x"], tile("xs", "xp", "r_x", [p - 1], "spread"))
    add(1, ["r_w2"], ("w12", TK, "w12", TK, TK, "r_w2", [7, 5, 6, 4], "far"))
    add(5, ["r_wd4"], tile("wd4", "wd4", "r_wd4", [7, 6], "far"))
    add(0, va, tile("a", "ao", "r_a", [2], "far"))
    add(4, va, tile("a", "ao", "r_a", [6], "far"))
    add(2, va, tile("a", "ao", "r_a", [0], "far"), tile("a", "ae", "r_ae", [3], "near"))
    add(6, va, tile("a", "ao", "r_a", [4], "far"), tile("a", "ae", "r_ae", [7], "near"))
    add(2, ["r_w1"], ("w12", TK, "w12", TK, TK, "r_w2", [3], "near"))
    for h in (0, 2, 4, 6):
        nm = "b0" if h < 4 else "b4"
        add(h, vb, tile("b", nm, "r_" + nm, list(to[h]), "far"), tile("b", nm, "r_" + nm, [h + 1], "near"))

    arrive = {}
    for r in range(N):
        for _, trs in calls[r]:
            for tr in trs:
                for d in tr[6]:
                    n = len(_bits(_engines(topo, cores, cores[r], cores[d], tr[7])))
                    arrive[(d, tr[5])] = arrive.get((d, tr[5]), 0) + n
    return calls, arrive


def rank_program(g, core, T, topo):
    r = T.rank_of(core)
    if r is None:
        return
    C, S = T.cores, T.sem
    calls, arrive = _plan(C, topo)
    even, low = r % 2 == 0, r < 4
    seen = set()

    def wait(q, qname, names):
        for nm in names:
            if (qname, nm) in seen:
                continue
            seen.add((qname, nm))
            val = 16 if nm.startswith("ld_") else arrive[(r, nm)] if nm.startswith("r_") else 1
            q.wait_ge(S[nm], val)

    def load(q, dst, src, lo, hi, sem):
        q.dma_start(T[dst][:, lo:hi], src[:, lo:hi]).then_inc(S[sem], 16)

    if r == 0:
        load(g.sync, "wus", T.wu, 2 * TK, 3 * TK, "ld_w2")
        load(g.sync, "wus", T.wu, 0, 2 * TK, "ld_w0")
        load(g.sync, "xs", T.x, 0, TK, "ld_x")
    elif r == 4:
        load(g.sync, "wds", T.wd, 0, TK, "ld_wd")
        load(g.scalar, "wus", T.wu, 0, 2 * TK, "ld_w0")
        load(g.sync, "xs", T.x, 0, TK, "ld_x")
    elif even:
        load(g.sync, "wds", T.wd, 0, TK, "ld_wd")
        load(g.scalar, "wus", T.wu, 0, TK, "ld_w0")
        load(g.sync, "xs", T.x, 0, TK, "ld_x")
    else:
        load(g.sync, "xs", T.x, 0, TK, "ld_x")
        load(g.sync, "wds", T.wd, 0, TK, "ld_wd")

    sent = 0
    for waits, trs in calls[r]:
        wait(g, "g", waits)
        ts = []
        for (sb, slo, db, dlo, w, sem, ranks, kind) in trs:
            masks = set(_engines(topo, C, core, C[d], kind) for d in ranks)
            assert len(masks) == 1 and all(topo.may_write(core, C[d]) for d in ranks)
            m = masks.pop()
            sent += len(_bits(m))
            ids = [topo.addr(C[d])[0:2] for d in ranks]
            ts.append((T[sb][:, slo:slo + w], T[db][:, dlo:dlo + w], S[sem], ids, m))
        if len(ts) == 1 and len(ts[0][3]) == 1:
            src, dst, sem, ids, m = ts[0]
            g.remote_dma(dst, src, sem, S.sent, ids[0][1], ids[0][0], m)
        else:
            g.remote_dma_fused(
                [RemoteDMATransfer(dst_ids=[DstId(rid=i[0], pnc=i[1]) for i in ids], dma_engine_mask=m,
                                   remote_sem=sem, srcs=[src], dsts=[dst for _ in ids], alu_op=0)
                 for (src, dst, sem, ids, m) in ts],
                local_sem=S.sent)
    g.wait_ge(S.sent, sent)

    g.vector.memset(T.zero[:], 0.0).then_inc(S.z, 1)
    wait(g.vector, "v", ["z"])
    bank = {"a": 0, "4": 0, "b": 2, "y": 2, "c": 4, "e": 6}

    def mm(grp, w, s, sdep, start=False, stop=False):
        for h in (0, 1):
            wait(g.tensor, "t", [w[2], "v_%s%d" % (sdep, h) if sdep in _STEPS else sdep])
            i = g.tensor.matmul(T["p%d" % (bank[grp] + h)][:, 0:HF], T[w[0]][:, w[1]:w[1] + HF],
                                T[s][:, h * HF:(h + 1) * HF], start=start, stop=stop)
            if stop:
                i.then_inc(S["m_%s%d" % (grp, h)], 1)

    def relu(grp, out):
        for h in (0, 1):
            wait(g.vector, "v", ["m_%s%d" % (grp, h)])
            g.vector.tensor_tensor(T[out][:, h * HF:(h + 1) * HF], T["p%d" % (bank[grp] + h)][:, 0:HF], T.zero[:],
                                   op=AluOpType.max).then_inc(S["v_%s%d" % (grp, h)], 1)

    def pair(buf, col, dep):
        return (buf, col, dep), (buf, col + HF, dep)

    U0, V0 = pair("wus", 0, "ld_w0")
    U1, V1 = pair("wus", TK, "ld_w0") if r % 4 == 0 else pair("w12", 0, "r_w1")
    U2, V2 = pair("wus", 2 * TK, "ld_w2") if r == 0 else pair("w12", TK, "r_w1" if r == 2 else "r_w2")
    D, E = pair("wds", 0, "ld_wd")
    D4, E4 = (D, E) if r == 4 else pair("wd4", 0, "r_wd4")
    De, Ee = (D, E) if even else pair("wde", 0, "r_wde")

    if even:
        mm("a", U0, "xs", "ld_x", start=True)
        mm("a", V0, "xp", "r_x", stop=True)
        relu("a", "a")
        if r % 4 == 2:
            mm("e", D, "a", "a", start=True)
        mine, other = (U1, V1) if r % 4 == 0 else (V1, U1)
        mm("b", mine, "a", "a", start=True)
        mm("b", other, "ao", "r_a", stop=True)
        relu("b", "b")
        bm, bmdep = "b", "b"
    else:
        mm("y", D, "xs", "ld_x", start=True)
        if r % 4 == 3:
            mm("e", De, "ae", "r_ae", start=True)
        bm = "b0" if low else "b4"
        bmdep = "r_" + bm
    bo = "b4" if low else "b0"
    Wm, Wo = (U2, V2) if low else (V2, U2)
    mm("c", Wm, bm, bmdep, start=True)
    if not low:
        mm("4", D4, bm, bmdep, start=True)
    mm("c", Wo, bo, "r_" + bo, stop=True)
    relu("c", "c")
    cur, step = "c", "c"
    if not low:
        mm("4", E4, cur, step, stop=True)
        relu("4", "y4")
        cur, step = "y4", "4"
    if r % 4 >= 2:
        mm("e", Ee, cur, step, stop=True)
        relu("e", "ye")
        cur, step = "ye", "e"
    if not even:
        mm("y", E, cur, step, stop=True)
        relu("y", "yo")
        cur, step = "yo", "y"

    wait(g.sync, "s", ["v_%s0" % step, "v_%s1" % step])
    g.sync.dma_start(T.y[:], T[cur][:]).then_inc(S.st, 16)
    g.sync.wait_ge(S.st, 16)
